import numpy as np, ml_dtypes
CORES = [7,15,23,31,167,175,183,191,327,335,343,351,487,495,503,511]
N = 16
def setup_inputs(rng):
    return {"x": rng.standard_normal((N, 128, 1024), dtype=np.float32).astype(ml_dtypes.bfloat16)}
def reference(x):
    s = x.sum(axis=0, dtype=np.float64).astype(x.dtype)
    b = 1024 // N
    return {"y": np.stack([s[:, r * b:(r + 1) * b] for r in range(N)])}

from concourse.bass import DstId, RemoteDMATransfer
from concourse.mybir import AluOpType

B = 64
SCRATCH = {
    "S": ("dram", [128, B], "bfloat16"),
    "L": ("dram", [2, 128, B], "bfloat16"),
}
SEMAPHORES = ["ld", "out", "cout", "yl", "acc",
              "arr0", "arr1", "arr2", "arr3", "cr0", "cr1", "cr2", "cr3"]


def _label(i):
    h, k = i // 4, i % 4
    rk = h >> 1
    col = h if rk == 0 else 3 - h
    return k | (col << 2) | (rk << 3)


def _rank(v):
    k, col, rk = v & 3, (v >> 2) & 1, v >> 3
    h = col if rk == 0 else 3 - col
    return 4 * h + k


def _gray(n):
    return n ^ (n >> 1)


def rank_program(g, core, T, topo):
    rank = T.rank_of(core)
    if rank is None:
        return
    v = _label(rank)
    sem = T.sem

    def step(t):
        p = _gray(16 - t)
        e = p ^ _gray(15 - t)
        return _rank(v ^ p), T.cores[_rank(v ^ e)], e.bit_length() - 1

    def load(t):
        d = step(t)[0]
        g.sync.dma_start(T.S[:], T.x[:, B * d:B * d + B]).then_inc(sem.ld, 16)

    g.scalar.dma_start(T.y[:], T.x[:, B * rank:B * rank + B]).then_inc(sem.yl, 16)
    load(1)

    n_arr = [0, 0, 0, 0]
    n_cr = [0, 0, 0, 0]
    n_cout = 0
    for t in range(1, 16):
        d, q, b = step(t)
        rid, pid = topo.addr(q, core)
        g.wait_ge(sem.ld, 16 * t)
        if t >= 2:
            pb = step(t - 1)[2]
            n_arr[pb] += 8
            g.wait_ge(sem["arr%d" % pb], n_arr[pb])
        if t >= 3:
            n_cr[b] += 1
            g.wait_ge(sem["cr%d" % b], n_cr[b])
        if t == 1:
            g.remote_dma(T.L[t % 2], T.S[:], sem["arr%d" % b], sem.out, pid, rid, 0xFF)
        else:
            g.remote_dma_fused([RemoteDMATransfer(
                dst_ids=[DstId(rid=rid, pnc=pid)], dma_engine_mask=0xFF, remote_sem=sem["arr%d" % b],
                srcs=[T.L[(t - 1) % 2], T.S[:]], dsts=[T.L[t % 2]], alu_op=1)], local_sem=sem.out)
        if t < 15:
            g.sync.wait_ge(sem.out, 8 * t)
            load(t + 1)
        g.wait_ge(sem.out, 8 * t)
        if 2 <= t < 15:
            _, q2, b2 = step(t + 1)
            rid2, pid2 = topo.addr(q2, core)
            g.remote_sem_update(sem["cr%d" % b2], sem.cout, pid2, rid2, 0x01)
            n_cout += 1

    n_arr[0] += 8
    g.wait_ge(sem.arr0, n_arr[0])
    g.wait_ge(sem.yl, 16)
    g.dma_start(T.y[:], T.L[1], accum_op=AluOpType.add, max_dma_last_dim=4096).then_inc(sem.acc, 16)
    g.wait_ge(sem.cout, n_cout)
    g.wait_ge(sem.acc, 16)
